import numpy as np
import ml_dtypes


def mxq(x, axis, fmt="e4m3"):
    dtype, down = {"e4m3": (ml_dtypes.float8_e4m3fn, 7), "e5m2": (ml_dtypes.float8_e5m2, 14)}[fmt]
    v = np.moveaxis(np.asarray(x, np.float32).astype(ml_dtypes.bfloat16).astype(np.float64), axis, -1)
    blocks = v.reshape(v.shape[:-1] + (-1, 32))
    amax = np.abs(blocks).max(-1, keepdims=True)
    byte = np.maximum(np.where(amax > 0, np.frexp(amax)[1] - 1 + 127, 0) - down, 1)
    scale = np.exp2(byte - 127.0)
    codes = (blocks / scale).astype(np.float32).astype(dtype).astype(np.float64)
    return np.moveaxis((codes * scale).reshape(v.shape), -1, axis)


WIDE = False


def mx_kscale(k):
    if not WIDE:
        return np.ones(k)
    levels = np.array([10, -10, 5, -5, 0])
    if k % 512:
        return np.exp2(np.random.permutation(np.resize(levels, k // 32))).repeat(32)
    a = np.empty((k // 512, 16))
    for p in range(k // 512):
        a[p, :8] = np.random.permutation(np.resize(levels, 8))
        for g in range(8):
            far = levels[np.abs(levels - a[p, g]) >= 10]
            a[p, g + 8] = far[np.random.randint(len(far))]
    return np.exp2(a.ravel()).repeat(32)


BF16 = ml_dtypes.bfloat16


def bf(x):
    return np.asarray(x, np.float32).astype(BF16)


def f64(x):
    return np.asarray(x).astype(np.float64)


E2M1 = np.array([0.0, 0.5, 1.0, 1.5, 2.0, 3.0, 4.0, 6.0, -0.0, -0.5, -1.0, -1.5, -2.0, -3.0, -4.0, -6.0])


def pack_weight(w, fmt):
    k, n = w.shape
    w = f64(bf(w)).reshape(k // 32, 32, n)
    amax = np.abs(w).max(1)
    if fmt == "e4m3":
        byte = np.frexp(amax)[1] - 1 + 127 - 7
    else:
        mant, ex = np.frexp(amax / 6.0)
        byte = np.where(mant > 0.5, ex, ex - 1) + 127
    byte = np.clip(np.where(amax > 0, byte, 1), 1, 254)
    scaled = (w * np.exp2(127.0 - byte)[:, None, :]).reshape(k, n).astype(np.float32)
    by_word = np.ascontiguousarray(scaled.reshape(k // 512, 128, 4, n).transpose(0, 1, 3, 2))
    if fmt == "e4m3":
        words = by_word.astype(ml_dtypes.float8_e4m3fn).view(np.uint8)
    else:
        c = by_word.astype(ml_dtypes.float4_e2m1fn).view(np.uint8) & 0xF
        words = c[..., 0::2] | (c[..., 1::2] << 4)
    return np.ascontiguousarray(words), np.ascontiguousarray(byte.astype(np.uint8).reshape(k // 512, 16, n))


def unpack_weight(words, scales, fmt):
    g, p, n, _ = words.shape
    if fmt == "e4m3":
        vals = np.ascontiguousarray(words).view(ml_dtypes.float8_e4m3fn).astype(np.float64)
    else:
        nib = np.empty((g, p, n, 4), np.uint8)
        nib[..., 0::2] = words & 0xF
        nib[..., 1::2] = words >> 4
        vals = E2M1[nib]
    vals = vals * np.repeat(np.exp2(scales.astype(np.float64) - 127.0), 8, axis=1)[..., None]
    return vals.transpose(0, 1, 3, 2).reshape(g * 512, n)
def pack4(w):
    words, scales = pack_weight(w, "e2m1")
    return words.reshape(words.shape[0], 128, -1), scales


def unpack4(words, scales):
    return unpack_weight(words.reshape(words.shape[0], 128, -1, 2), scales, "e2m1")


def planes(Y):
    n, m = Y.shape
    b = f64(bf(Y)).reshape(n // 32, 32, m)
    amax = np.abs(b).max(1)
    byte = np.clip(np.where(amax > 0, np.frexp(amax)[1] - 1 + 127 - 7, 1), 1, 254)
    codes = (b * np.exp2(127.0 - byte)[:, None, :]).reshape(n, m).astype(np.float32).astype(ml_dtypes.float8_e4m3fn).view(np.uint8)
    words = codes.reshape(n // 512, 128, 4, m).transpose(0, 1, 3, 2)
    return np.ascontiguousarray(words), np.ascontiguousarray(byte.astype(np.uint8).reshape(n // 512, 16, m))


I, F, D = 1536, 1024, 512


def setup_inputs():
    s = mx_kscale(I)
    t = mx_kscale(F)
    strength = np.exp(0.8 * np.random.randn(I))
    edges = np.random.rand(I, I) < 0.6
    adj = 0.25 * edges * (0.5 + np.random.rand(I, I)) * strength[None, :]
    adj_words, adj_scales = pack4(adj * s[:, None])
    deg = (unpack4(adj_words, adj_scales) / s[:, None]).sum(axis=0)
    x = np.random.randn(I, F) * t[None, :] / s[:, None]
    w = 2.0 * np.random.randn(F, D) / np.sqrt(F)
    w_words, w_scales = pack4(w / t[:, None])
    e = strength[:, None] * np.random.randn(I, D)
    return {"adj_words": adj_words, "adj_scales": adj_scales,
            "x": bf(x), "deg_scale": bf(1.0 / np.sqrt(deg)),
            "w_words": w_words, "w_scales": w_scales,
            "b": bf(0.3 * np.random.randn(D)), "e": bf(e)}

def reference(adj_words, adj_scales, x, deg_scale, w_words, w_scales, b, e):
    S = unpack4(adj_words, adj_scales)
    W = unpack4(w_words, w_scales)
    H = (S.T @ mxq(f64(x), 0, "e4m3")) * f64(deg_scale)[:, None]
    Z = mxq(H, 1, "e4m3") @ W
    y = np.maximum(Z + f64(b)[None, :], 0.0) + f64(e)
    Y = y.reshape(I, D)
    words, scales = planes(Y)
    return y, words, scales

@@ -1,0 +1,393 @@
+from contextlib import ExitStack
+
+import concourse.mybir as mybir
+from concourse.masks import make_identity
+
+I, F, D = 1536, 1024, 512
+FLOPS = 2 * I * I * F + 2 * I * F * D
+
+F32 = mybir.dt.float32
+BF16 = mybir.dt.bfloat16
+I32 = mybir.dt.int32
+U32 = mybir.dt.uint32
+U8 = mybir.dt.uint8
+FP8X4 = mybir.dt.float8_e4m3fn_x4
+FP4X4 = mybir.dt.float4_e2m1fn_x4
+ALU = mybir.AluOpType
+ACT = mybir.ActivationFunctionType
+
+P = 128
+K = 512
+NG = I // K
+NF = F // K
+ROW_UNITS = [(0, 0), (2, 0)]
+
+
+def tile_item_graph_propagation_h1_kernel(
+    tc, adj_words, adj_scales, x, deg_scale, w_words, w_scales, b, e, out_0, out_1, out_2
+):
+    nc = tc.nc
+    with ExitStack() as ctx:
+        sb = ctx.enter_context(tc.tile_pool(name="sb", bufs=1))
+        ps = ctx.enter_context(tc.psum_pool(name="ps", bufs=1))
+        ctx.enter_context(tc.manual_schedule())
+
+        def sbuf(name, shape, dtype):
+            return sb.tile(shape, dtype, name=name, align_bytes=64)
+
+        bank = [ps.tile([P, 512], F32, name="bank%d" % i) for i in range(8)]
+        pairs = [(fg, c) for fg in range(NF) for c in range(NG)]
+        x_raw = {k: sbuf("x_raw%d%d" % k, [P, 4, K], BF16) for k in pairs}
+        x_il = {k: sbuf("x_il%d%d" % k, [P, 4 * K], BF16) for k in pairs}
+        x_codes = {k: sbuf("x_codes%d%d" % k, [P, K], U32) for k in pairs}
+        x_scales = {k: sbuf("x_scales%d%d" % k, [P, K], U8) for k in pairs}
+        s_words = [sbuf("s_words%d" % g, [P, NG, 2 * K], U8) for g in range(NG)]
+        s_scales_first = sbuf("s_scales_first", [P, NG, 2 * K], U8)
+        s_scales_rest = sbuf("s_scales_rest", [P, NG, K], U8)
+        w_codes = sbuf("w_codes", [P, NF, 2 * D], U8)
+        w_plane = sbuf("w_plane", [P, NF, D], U8)
+        vec_rows = sbuf("vec_rows", [P, P], BF16)
+        vec_cols = sbuf("vec_cols", [P, 16], BF16)
+        deg_cols = sbuf("deg_cols", [P, 16], F32)
+        vec_all = sbuf("vec_all", [P, I + D], BF16)
+        ident_bf = sbuf("ident_bf", [P, P], BF16)
+        ident_f32 = sbuf("ident_f32", [P, P], F32)
+        units = [(g, fg) for g in range(NG) for fg in range(NF)]
+        h_il = {k: sbuf("h_il%d%d" % k, [P, 4 * K], BF16) for k in units}
+        h_codes = {k: sbuf("h_codes%d%d" % k, [P, K], U32) for k in units}
+        h_scales = {k: sbuf("h_scales%d%d" % k, [P, K], U8) for k in units}
+        h_rows = {k: [sbuf("h_rows%d%d%d" % (k + (a,)), [P, K], BF16) for a in range(4)] for k in ROW_UNITS}
+        e_sb = [sbuf("e_sb%d" % g, [P, 4, D], BF16) for g in range(NG)]
+        y_sb = [sbuf("y_sb%d" % g, [P, 4, D], F32) for g in range(NG)]
+        y_il = [sbuf("y_il%d" % g, [P, 4 * D], BF16) for g in range(NG)]
+        y_codes = [sbuf("y_codes%d" % g, [P, D], U32) for g in range(NG)]
+        y_scales = [sbuf("y_scales%d" % g, [P, D], U8) for g in range(NG)]
+
+        def s_operand(g, c, a):
+            words = s_words[g][:, c, 2 * P * a : 2 * P * (a + 1)].bitcast(FP4X4)
+            if g < 2:
+                n0 = K * g + P * a
+                scales = s_scales_first[:, c, n0 : n0 + P]
+            else:
+                scales = s_scales_rest[:, c, P * a : P * (a + 1)]
+            return words, scales
+
+        def copy_on(eng, out, in_):
+            if eng == "V":
+                nc.vector.tensor_copy(out=out, in_=in_)
+            else:
+                nc.scalar.copy(out=out, in_=in_)
+
+        def setup():
+            nc.vector.memset(vec_rows[:], 0.0)
+            nc.vector.memset(s_scales_first[:].bitcast(I32), 0)
+            nc.vector.memset(s_scales_rest[:].bitcast(I32), 0)
+            nc.vector.memset(w_plane[:].bitcast(I32), 0)
+            nc.scalar.dma_start(out=vec_rows[0:12, :], in_=deg_scale.rearrange("(a p) -> a p", p=P))
+            nc.scalar.dma_start(out=vec_rows[12:16, :], in_=b.rearrange("(a p) -> a p", p=P))
+            make_identity(nc, ident_bf[:])
+            nc.scalar.activation(out=ident_f32[:], in_=ident_bf[:], func=ACT.Copy)
+
+        def load_x(fg, c):
+            src = x[K * c : K * (c + 1), K * fg : K * (fg + 1)]
+            nc.sync.dma_start(out=x_raw[fg, c][:], in_=src.rearrange("(p j) f -> p j f", j=4))
+
+        def load_s_words(g):
+            src = adj_words[:, :, 2 * K * g : 2 * K * (g + 1)].rearrange("c p n -> p c n")
+            nc.sync.dma_start(out=s_words[g][:].bitcast(I32), in_=src.bitcast(I32))
+
+        def load_plane(plane, src):
+            for q in range(4):
+                rows = src[:, 4 * q : 4 * q + 4, :].rearrange("c r n -> r c n")
+                nc.sync.dma_start(out=plane[32 * q : 32 * q + 4, :, :].bitcast(I32), in_=rows.bitcast(I32))
+
+        def load_s_scales_first():
+            load_plane(s_scales_first, adj_scales[:, :, 0 : 2 * K])
+
+        def load_s_scales_rest():
+            load_plane(s_scales_rest, adj_scales[:, :, 2 * K : I])
+
+        def load_w():
+            nc.sync.dma_start(out=w_codes[:].bitcast(I32), in_=w_words.rearrange("c p n -> p c n").bitcast(I32))
+            load_plane(w_plane, w_scales)
+
+        def load_e(g):
+            nc.sync.dma_start(out=e_sb[g][:], in_=e[K * g : K * (g + 1), :].rearrange("(p t) d -> p t d", t=4))
+
+        def x_interleave(fg, c, eng, t0, t1):
+            out = x_il[fg, c][:, K * t0 : K * t1].rearrange("p (t n h j) -> p n t h j", n=64, h=2, j=4)
+            src = x_raw[fg, c][:].rearrange("p j (n h t) -> p n t h j", h=2, t=4)[:, :, t0:t1, :, :]
+            copy_on(eng, out, src)
+
+        def x_quantize(fg, c):
+            nc.vector.quantize_mx(out=x_codes[fg, c][:].bitcast(FP8X4), scales=x_scales[fg, c][:], in_=x_il[fg, c][:])
+
+        def vec_turn(bk):
+            nc.tensor.transpose(bank[bk][:].bitcast(BF16)[:, 0:P], vec_rows[:], ident_bf[:])
+
+        def vec_turn_out(bk):
+            nc.scalar.copy(out=deg_cols[:], in_=bank[bk][:].bitcast(BF16)[:, 0:16])
+            nc.scalar.copy(out=vec_cols[:], in_=bank[bk][:].bitcast(BF16)[:, 0:16])
+
+        def vec_spread(half, bk):
+            for i in range(8):
+                col = vec_cols[:, 8 * half + i : 8 * half + i + 1].to_broadcast([P, P])
+                nc.tensor.transpose(bank[bk][:].bitcast(BF16)[:, P * i : P * (i + 1)], col, ident_bf[:])
+
+        def vec_spread_out(half, bk):
+            nc.scalar.copy(out=vec_all[:, 1024 * half : 1024 * (half + 1)], in_=bank[bk][:].bitcast(BF16))
+
+        def cols_matmul(g, fg, a, bk):
+            for j in range(4):
+                for c in range(NG):
+                    words, scales = s_operand(g, c, a)
+                    nc.tensor.matmul_mx(
+                        out=bank[bk][:, P * j : P * (j + 1)],
+                        lhsT=x_codes[fg, c][:, P * j : P * (j + 1)].bitcast(FP8X4),
+                        lhsT_scale=x_scales[fg, c][:, P * j : P * (j + 1)],
+                        rhs=words,
+                        rhs_scale=scales,
+                        start=(c == 0),
+                        stop=(c == NG - 1),
+                    )
+
+        def cols_out(g, fg, a, bk):
+            out = h_il[g, fg][:].rearrange("p (t m j) -> p t m j", t=4, j=4)[:, :, 32 * a : 32 * (a + 1), :]
+            acc = bank[bk][:].rearrange("p (j m t) -> p t m j", j=4, t=4)
+            n0 = K * g + P * a
+            deg = vec_all[:, n0 : n0 + P].rearrange("p (m t o) -> p t m o", t=4, o=1).to_broadcast([P, 4, 32, 4])
+            nc.vector.tensor_tensor(out=out, in0=acc, in1=deg, op=ALU.mult)
+
+        def rows_matmul(g, fg, a, c, bk):
+            words, scales = s_operand(g, c, a)
+            nc.tensor.matmul_mx(
+                out=bank[bk][:],
+                lhsT=words,
+                lhsT_scale=scales,
+                rhs=x_codes[fg, c][:].bitcast(FP8X4),
+                rhs_scale=x_scales[fg, c][:],
+                start=(c == 0),
+                stop=(c == NG - 1),
+            )
+
+        def rows_out(g, fg, a, bk, eng):
+            out = h_rows[g, fg][a][:].rearrange("p (u m v) -> p u m v", u=2, v=2)
+            acc = bank[bk][:].rearrange("p (u v m) -> p u m v", u=2, v=2)
+            deg = deg_cols[:, 4 * g + a : 4 * g + a + 1]
+            if eng == "V":
+                nc.vector.tensor_scalar(out=out, in0=acc, scalar1=deg, scalar2=None, op0=ALU.mult)
+            else:
+                nc.scalar.activation(out=out, in_=acc, func=ACT.Copy, scale=deg)
+
+        def rows_turn(g, fg, half, bk):
+            for a2 in range(2):
+                words = h_rows[g, fg][2 * half + a2][:].bitcast(F32)
+                for u in range(2):
+                    n0 = 2 * P * u + P * a2
+                    nc.tensor.transpose(bank[bk][:, n0 : n0 + P], words[:, P * u : P * (u + 1)], ident_f32[:])
+
+        def rows_turn_out(g, fg, half, bk, eng):
+            out = h_il[g, fg][:].bitcast(F32).rearrange("p (t m u) -> p t m u", t=4, u=2)[:, :, 64 * half : 64 * (half + 1), :]
+            copy_on(eng, out, bank[bk][:].rearrange("p (u m t) -> p t m u", u=2, t=4))
+
+        def h_quantize(g, fg, t0, t1):
+            nc.vector.quantize_mx(
+                out=h_codes[g, fg][:, P * t0 : P * t1].bitcast(FP8X4),
+                scales=h_scales[g, fg][:, P * t0 : P * t1],
+                in_=h_il[g, fg][:, K * t0 : K * t1],
+            )
+
+        def layer_matmul(g, t, fg, bk):
+            nc.tensor.matmul_mx(
+                out=bank[bk][:],
+                lhsT=h_codes[g, fg][:, P * t : P * (t + 1)].bitcast(FP8X4),
+                lhsT_scale=h_scales[g, fg][:, P * t : P * (t + 1)],
+                rhs=w_codes[:, fg, :].bitcast(FP4X4),
+                rhs_scale=w_plane[:, fg, :],
+                start=(fg == 0),
+                stop=(fg == NF - 1),
+            )
+
+        def bias_out(g, t, bk, d0=0, d1=D):
+            nc.vector.tensor_tensor(out=y_sb[g][:, t, d0:d1], in0=bank[bk][:, d0:d1], in1=vec_all[:, I + d0 : I + d1], op=ALU.add)
+
+        def relu_add(g, t0, t1, d0, d1):
+            y = y_sb[g][:, t0:t1, d0:d1]
+            nc.vector.scalar_tensor_tensor(out=y, in0=y, scalar=0.0, in1=e_sb[g][:, t0:t1, d0:d1], op0=ALU.max, op1=ALU.add)
+
+        def y_interleave(g, d0, d1, eng):
+            out = y_il[g][:, 4 * d0 : 4 * d1].rearrange("p (n i t) -> p n t i", i=4, t=4)
+            copy_on(eng, out, y_sb[g][:, :, d0:d1].rearrange("p t (n i) -> p n t i", i=4))
+
+        def y_quantize(g, d0, d1):
+            nc.vector.quantize_mx(
+                out=y_codes[g][:, d0:d1].bitcast(FP8X4), scales=y_scales[g][:, d0:d1], in_=y_il[g][:, 4 * d0 : 4 * d1]
+            )
+
+        def store_y(g, d0, d1):
+            dst = out_0[K * g : K * (g + 1), d0:d1].rearrange("(p t) d -> p t d", t=4)
+            nc.sync.dma_start(out=dst, in_=y_sb[g][:, :, d0:d1])
+
+        def store_codes(g, d0, d1):
+            dst = out_1[g].rearrange("p m t -> p (m t)")[:, 4 * d0 : 4 * d1]
+            nc.sync.dma_start(out=dst.bitcast(I32), in_=y_codes[g][:, d0:d1].bitcast(I32))
+
+        def store_scales(g, q, eng):
+            queue = nc.sync if eng == "SP" else nc.scalar
+            queue.dma_start(out=out_2[g, 4 * q : 4 * q + 4, :].bitcast(I32), in_=y_scales[g][32 * q : 32 * q + 4, :].bitcast(I32))
+
+
+        setup()
+        load_x(0, 0)
+        load_s_words(0)
+        load_s_scales_first()
+        load_x(0, 1)
+        load_x(0, 2)
+        load_s_words(1)
+        for c in range(NG):
+            load_x(1, c)
+        load_w()
+        load_e(0)
+        load_s_words(2)
+        load_s_scales_rest()
+        load_e(1)
+        load_e(2)
+
+        vec_turn(7)
+        vec_turn_out(7)
+        vec_spread(0, 6)
+        x_interleave(0, 0, "V", 0, 3)
+        x_interleave(0, 0, "S", 3, 4)
+        x_quantize(0, 0)
+        vec_spread_out(0, 6)
+        x_interleave(0, 1, "V", 0, 2)
+        x_interleave(0, 1, "S", 2, 4)
+        x_quantize(0, 1)
+        x_interleave(0, 2, "V", 0, 2)
+        x_interleave(0, 2, "S", 2, 4)
+        x_quantize(0, 2)
+        for c in range(NG):
+            for a in range(4):
+                rows_matmul(0, 0, a, c, a)
+            if c == 0:
+                vec_spread(1, 7)
+                vec_spread_out(1, 7)
+        for a in range(4):
+            cols_matmul(1, 0, a, 4 + a)
+        x_interleave(1, 0, "V", 0, 2)
+        x_interleave(1, 0, "S", 2, 4)
+        x_interleave(1, 1, "V", 0, 2)
+        x_interleave(1, 1, "S", 2, 4)
+        x_quantize(1, 0)
+        x_quantize(1, 1)
+        x_interleave(1, 2, "V", 0, 3)
+        x_interleave(1, 2, "S", 3, 4)
+        x_quantize(1, 2)
+        for a in range(4):
+            rows_out(0, 0, a, a, "S")
+        for a in range(4):
+            cols_out(1, 0, a, 4 + a)
+        cols_matmul(0, 1, 0, 0)
+        cols_matmul(0, 1, 1, 1)
+        rows_turn(0, 0, 0, 2)
+        rows_turn(0, 0, 1, 3)
+        rows_turn_out(0, 0, 0, 2, "S")
+        rows_turn_out(0, 0, 1, 3, "S")
+        cols_out(0, 1, 0, 0)
+        h_quantize(1, 0, 0, 4)
+        cols_out(0, 1, 1, 1)
+        cols_matmul(0, 1, 2, 4)
+        cols_matmul(0, 1, 3, 5)
+        h_quantize(0, 0, 0, 4)
+        cols_out(0, 1, 2, 4)
+        cols_out(0, 1, 3, 5)
+
+        cols_matmul(1, 1, 0, 6)
+        for t, bk in enumerate([7, 0, 1, 2]):
+            layer_matmul(0, t, 0, bk)
+        h_quantize(0, 1, 0, 4)
+        for t, bk in enumerate([7, 0, 1, 2]):
+            layer_matmul(0, t, 1, bk)
+        cols_out(1, 1, 0, 6)
+        bias_out(0, 0, 7)
+        bias_out(0, 1, 0)
+        cols_matmul(1, 1, 1, 3)
+        cols_matmul(1, 1, 2, 4)
+        cols_matmul(1, 1, 3, 5)
+        bias_out(0, 2, 1)
+        cols_out(1, 1, 1, 3)
+        bias_out(0, 3, 2)
+        cols_out(1, 1, 2, 4)
+        relu_add(0, 0, 1, 0, 512)
+        cols_out(1, 1, 3, 5)
+        for a, bk in [(0, 6), (1, 7)]:
+            for c in range(NG):
+                rows_matmul(2, 0, a, c, bk)
+            rows_out(2, 0, a, bk, "S")
+        relu_add(0, 1, 2, 0, 512)
+        for t, bk in enumerate([0, 1, 2, 3]):
+            layer_matmul(1, t, 0, bk)
+        h_quantize(1, 1, 0, 4)
+        for t, bk in enumerate([0, 1, 2, 3]):
+            layer_matmul(1, t, 1, bk)
+        relu_add(0, 2, 4, 0, 512)
+        store_y(0, 0, 512)
+        y_interleave(0, 0, 512, "S")
+        for a, bk in [(2, 4), (3, 5)]:
+            for c in range(NG):
+                rows_matmul(2, 0, a, c, bk)
+            rows_out(2, 0, a, bk, "S")
+        for t, bk in enumerate([0, 1, 2, 3]):
+            bias_out(1, t, bk)
+        relu_add(1, 0, 2, 0, 512)
+        cols_matmul(2, 1, 0, 6)
+        cols_matmul(2, 1, 1, 7)
+        rows_turn(2, 0, 0, 0)
+        rows_turn(2, 0, 1, 1)
+        rows_turn_out(2, 0, 0, 0, "S")
+        rows_turn_out(2, 0, 1, 1, "S")
+        cols_matmul(2, 1, 2, 2)
+        cols_matmul(2, 1, 3, 3)
+        relu_add(1, 2, 4, 0, 512)
+        store_y(1, 0, 512)
+        y_interleave(1, 0, 512, "S")
+        cols_out(2, 1, 0, 6)
+        y_quantize(0, 0, 512)
+        store_codes(0, 0, 512)
+        for q in range(4):
+            store_scales(0, q, "SP")
+        cols_out(2, 1, 1, 7)
+        h_quantize(2, 0, 0, 4)
+        cols_out(2, 1, 2, 2)
+        cols_out(2, 1, 3, 3)
+
+        last = [4, 5, 0, 1]
+        for t, bk in enumerate(last):
+            layer_matmul(2, t, 0, bk)
+        for t, bk in enumerate(last):
+            h_quantize(2, 1, t, t + 1)
+            layer_matmul(2, t, 1, bk)
+        y_quantize(1, 0, 512)
+        store_codes(1, 0, 512)
+        for q in range(4):
+            store_scales(1, q, "SP")
+        for t, bk in enumerate(last):
+            bias_out(2, t, bk, 0, 256)
+        bias_out(2, 0, last[0], 256, 512)
+        relu_add(2, 0, 4, 0, 256)
+        store_y(2, 0, 256)
+        y_interleave(2, 0, 256, "S")
+        for t in range(1, 4):
+            bias_out(2, t, last[t], 256, 512)
+        chunks = [(256, 384), (384, 448), (448, 512)]
+        for d0, d1 in chunks:
+            relu_add(2, 0, 4, d0, d1)
+            y_interleave(2, d0, d1, "S")
+        store_y(2, 256, 512)
+        y_quantize(2, 0, 256)
+        store_codes(2, 0, 256)
+        for d0, d1 in chunks:
+            y_quantize(2, d0, d1)
+        store_codes(2, 256, 512)
+        for q in range(4):
+            store_scales(2, q, "SP" if q < 2 else "S")

@@ -20,7 +20,7 @@ P = 128
 K = 512
 NG = I // K
 NF = F // K
-ROW_UNITS = [(0, 0), (2, 0)]
+ROW_UNITS = [(0, 0), (1, 1), (2, 0)]
 
 
 def tile_item_graph_propagation_h1_kernel(
@@ -42,8 +42,7 @@ def tile_item_graph_propagation_h1_kernel(
         x_codes = {k: sbuf("x_codes%d%d" % k, [P, K], U32) for k in pairs}
         x_scales = {k: sbuf("x_scales%d%d" % k, [P, K], U8) for k in pairs}
         s_words = [sbuf("s_words%d" % g, [P, NG, 2 * K], U8) for g in range(NG)]
-        s_scales_first = sbuf("s_scales_first", [P, NG, 2 * K], U8)
-        s_scales_rest = sbuf("s_scales_rest", [P, NG, K], U8)
+        s_scales = [sbuf("s_scales%d" % g, [P, NG, K], U8) for g in range(NG)]
         w_codes = sbuf("w_codes", [P, NF, 2 * D], U8)
         w_plane = sbuf("w_plane", [P, NF, D], U8)
         vec_rows = sbuf("vec_rows", [P, P], BF16)
@@ -57,6 +56,7 @@ def tile_item_graph_propagation_h1_kernel(
         h_codes = {k: sbuf("h_codes%d%d" % k, [P, K], U32) for k in units}
         h_scales = {k: sbuf("h_scales%d%d" % k, [P, K], U8) for k in units}
         h_rows = {k: [sbuf("h_rows%d%d%d" % (k + (a,)), [P, K], BF16) for a in range(4)] for k in ROW_UNITS}
+        r_cols = [sbuf("r_cols%d" % dt, [P, K], F32) for dt in range(4)]
         e_sb = [sbuf("e_sb%d" % g, [P, 4, D], BF16) for g in range(NG)]
         y_sb = [sbuf("y_sb%d" % g, [P, 4, D], F32) for g in range(NG)]
         y_il = [sbuf("y_il%d" % g, [P, 4 * D], BF16) for g in range(NG)]
@@ -65,12 +65,7 @@ def tile_item_graph_propagation_h1_kernel(
 
         def s_operand(g, c, a):
             words = s_words[g][:, c, 2 * P * a : 2 * P * (a + 1)].bitcast(FP4X4)
-            if g < 2:
-                n0 = K * g + P * a
-                scales = s_scales_first[:, c, n0 : n0 + P]
-            else:
-                scales = s_scales_rest[:, c, P * a : P * (a + 1)]
-            return words, scales
+            return words, s_scales[g][:, c, P * a : P * (a + 1)]
 
         def copy_on(eng, out, in_):
             if eng == "V":
@@ -80,10 +75,12 @@ def tile_item_graph_propagation_h1_kernel(
 
         def setup():
             nc.vector.memset(vec_rows[:], 0.0)
-            nc.vector.memset(s_scales_first[:].bitcast(I32), 0)
-            nc.vector.memset(s_scales_rest[:].bitcast(I32), 0)
+            for plane in s_scales:
+                nc.vector.memset(plane[:].bitcast(I32), 0)
             nc.vector.memset(w_plane[:].bitcast(I32), 0)
-            nc.scalar.dma_start(out=vec_rows[0:12, :], in_=deg_scale.rearrange("(a p) -> a p", p=P))
+            deg_rows = deg_scale.rearrange("(a p) -> a p", p=P)
+            nc.scalar.dma_start(out=vec_rows[0:8, :], in_=deg_rows[0:8, :])
+            nc.scalar.dma_start(out=vec_rows[8:12, :], in_=deg_rows[8:12, :])
             nc.scalar.dma_start(out=vec_rows[12:16, :], in_=b.rearrange("(a p) -> a p", p=P))
             make_identity(nc, ident_bf[:])
             nc.scalar.activation(out=ident_f32[:], in_=ident_bf[:], func=ACT.Copy)
@@ -101,11 +98,11 @@ def tile_item_graph_propagation_h1_kernel(
                 rows = src[:, 4 * q : 4 * q + 4, :].rearrange("c r n -> r c n")
                 nc.sync.dma_start(out=plane[32 * q : 32 * q + 4, :, :].bitcast(I32), in_=rows.bitcast(I32))
 
-        def load_s_scales_first():
-            load_plane(s_scales_first, adj_scales[:, :, 0 : 2 * K])
+        def load_s_scales(g):
+            load_plane(s_scales[g], adj_scales[:, :, K * g : K * (g + 1)])
 
-        def load_s_scales_rest():
-            load_plane(s_scales_rest, adj_scales[:, :, 2 * K : I])
+        def load_spread(n0, vec):
+            nc.sync.dma_start(out=vec_all[:, n0 : n0 + K], in_=vec.partition_broadcast(P))
 
         def load_w():
             nc.sync.dma_start(out=w_codes[:].bitcast(I32), in_=w_words.rearrange("c p n -> p c n").bitcast(I32))
@@ -129,13 +126,13 @@ def tile_item_graph_propagation_h1_kernel(
             nc.scalar.copy(out=deg_cols[:], in_=bank[bk][:].bitcast(BF16)[:, 0:16])
             nc.scalar.copy(out=vec_cols[:], in_=bank[bk][:].bitcast(BF16)[:, 0:16])
 
-        def vec_spread(half, bk):
-            for i in range(8):
-                col = vec_cols[:, 8 * half + i : 8 * half + i + 1].to_broadcast([P, P])
+        def vec_spread(c0, c1, bk):
+            for i in range(c1 - c0):
+                col = vec_cols[:, c0 + i : c0 + i + 1].to_broadcast([P, P])
                 nc.tensor.transpose(bank[bk][:].bitcast(BF16)[:, P * i : P * (i + 1)], col, ident_bf[:])
 
-        def vec_spread_out(half, bk):
-            nc.scalar.copy(out=vec_all[:, 1024 * half : 1024 * (half + 1)], in_=bank[bk][:].bitcast(BF16))
+        def vec_spread_out(c0, c1, bk):
+            nc.scalar.copy(out=vec_all[:, P * c0 : P * c1], in_=bank[bk][:].bitcast(BF16)[:, 0 : P * (c1 - c0)])
 
         def cols_matmul(g, fg, a, bk):
             for j in range(4):
@@ -215,6 +212,29 @@ def tile_item_graph_propagation_h1_kernel(
             y = y_sb[g][:, t0:t1, d0:d1]
             nc.vector.scalar_tensor_tensor(out=y, in0=y, scalar=0.0, in1=e_sb[g][:, t0:t1, d0:d1], op0=ALU.max, op1=ALU.add)
 
+        def layer_t_matmul(g, dt, fg, bk):
+            nc.tensor.matmul_mx(
+                out=bank[bk][:],
+                lhsT=w_codes[:, fg, 2 * P * dt : 2 * P * (dt + 1)].bitcast(FP4X4),
+                lhsT_scale=w_plane[:, fg, P * dt : P * (dt + 1)],
+                rhs=h_codes[g, fg][:].bitcast(FP8X4),
+                rhs_scale=h_scales[g, fg][:],
+                start=(fg == 0),
+                stop=(fg == NF - 1),
+            )
+
+        def layer_t_out(dt, bk):
+            nc.scalar.activation(out=r_cols[dt][:], in_=bank[bk][:], func=ACT.Relu, bias=deg_cols[:, 12 + dt : 13 + dt])
+
+        def layer_t_turn(dt, bk):
+            for t in range(4):
+                nc.tensor.transpose(bank[bk][:, P * t : P * (t + 1)], r_cols[dt][:, P * t : P * (t + 1)], ident_f32[:])
+
+        def add_out(g, dt, bk):
+            cols = slice(P * dt, P * (dt + 1))
+            acc = bank[bk][:].rearrange("p (t d) -> p t d", t=4)
+            nc.vector.tensor_tensor(out=y_sb[g][:, :, cols], in0=acc, in1=e_sb[g][:, :, cols], op=ALU.add)
+
         def y_interleave(g, d0, d1, eng):
             out = y_il[g][:, 4 * d0 : 4 * d1].rearrange("p (n i t) -> p n t i", i=4, t=4)
             copy_on(eng, out, y_sb[g][:, :, d0:d1].rearrange("p t (n i) -> p n t i", i=4))
@@ -240,48 +260,43 @@ def tile_item_graph_propagation_h1_kernel(
         setup()
         load_x(0, 0)
         load_s_words(0)
-        load_s_scales_first()
+        load_s_scales(0)
         load_x(0, 1)
         load_x(0, 2)
         load_s_words(1)
+        load_s_scales(1)
         for c in range(NG):
             load_x(1, c)
         load_w()
+        load_spread(I, b)
         load_e(0)
         load_s_words(2)
-        load_s_scales_rest()
+        load_s_scales(2)
+        load_spread(2 * K, deg_scale[2 * K : I])
         load_e(1)
         load_e(2)
 
         vec_turn(7)
         vec_turn_out(7)
-        vec_spread(0, 6)
+        vec_spread(0, 8, 7)
         x_interleave(0, 0, "V", 0, 3)
         x_interleave(0, 0, "S", 3, 4)
         x_quantize(0, 0)
-        vec_spread_out(0, 6)
-        x_interleave(0, 1, "V", 0, 2)
-        x_interleave(0, 1, "S", 2, 4)
-        x_quantize(0, 1)
-        x_interleave(0, 2, "V", 0, 2)
-        x_interleave(0, 2, "S", 2, 4)
-        x_quantize(0, 2)
+        for c in range(1, NG):
+            x_interleave(0, c, "V", 0, 2)
+            x_interleave(0, c, "S", 2, 4)
+            x_quantize(0, c)
+        vec_spread_out(0, 8, 7)
         for c in range(NG):
             for a in range(4):
                 rows_matmul(0, 0, a, c, a)
-            if c == 0:
-                vec_spread(1, 7)
-                vec_spread_out(1, 7)
         for a in range(4):
             cols_matmul(1, 0, a, 4 + a)
-        x_interleave(1, 0, "V", 0, 2)
-        x_interleave(1, 0, "S", 2, 4)
-        x_interleave(1, 1, "V", 0, 2)
-        x_interleave(1, 1, "S", 2, 4)
-        x_quantize(1, 0)
-        x_quantize(1, 1)
-        x_interleave(1, 2, "V", 0, 3)
-        x_interleave(1, 2, "S", 3, 4)
+        for c in range(NG):
+            x_interleave(1, c, "V", 0, 2)
+            x_interleave(1, c, "S", 2, 4)
+            if c > 0:
+                x_quantize(1, c - 1)
         x_quantize(1, 2)
         for a in range(4):
             rows_out(0, 0, a, a, "S")
@@ -302,92 +317,101 @@ def tile_item_graph_propagation_h1_kernel(
         cols_out(0, 1, 2, 4)
         cols_out(0, 1, 3, 5)
 
-        cols_matmul(1, 1, 0, 6)
+        def rows_bank(g, fg, a, bk):
+            for c in range(NG):
+                rows_matmul(g, fg, a, c, bk)
+            rows_out(g, fg, a, bk, "S")
+
+        rows_bank(1, 1, 0, 6)
         for t, bk in enumerate([7, 0, 1, 2]):
             layer_matmul(0, t, 0, bk)
         h_quantize(0, 1, 0, 4)
         for t, bk in enumerate([7, 0, 1, 2]):
             layer_matmul(0, t, 1, bk)
-        cols_out(1, 1, 0, 6)
-        bias_out(0, 0, 7)
-        bias_out(0, 1, 0)
-        cols_matmul(1, 1, 1, 3)
+            bias_out(0, t, bk)
+        rows_bank(1, 1, 1, 3)
         cols_matmul(1, 1, 2, 4)
-        cols_matmul(1, 1, 3, 5)
-        bias_out(0, 2, 1)
-        cols_out(1, 1, 1, 3)
-        bias_out(0, 3, 2)
-        cols_out(1, 1, 2, 4)
+        rows_turn(1, 1, 0, 5)
+        rows_turn_out(1, 1, 0, 5, "S")
+        cols_matmul(1, 1, 3, 6)
         relu_add(0, 0, 1, 0, 512)
-        cols_out(1, 1, 3, 5)
-        for a, bk in [(0, 6), (1, 7)]:
-            for c in range(NG):
-                rows_matmul(2, 0, a, c, bk)
-            rows_out(2, 0, a, bk, "S")
+        cols_out(1, 1, 2, 4)
         relu_add(0, 1, 2, 0, 512)
+        cols_out(1, 1, 3, 6)
+        relu_add(0, 2, 3, 0, 512)
+        rows_bank(2, 0, 0, 7)
         for t, bk in enumerate([0, 1, 2, 3]):
             layer_matmul(1, t, 0, bk)
         h_quantize(1, 1, 0, 4)
-        for t, bk in enumerate([0, 1, 2, 3]):
-            layer_matmul(1, t, 1, bk)
-        relu_add(0, 2, 4, 0, 512)
+        relu_add(0, 3, 4, 0, 512)
         store_y(0, 0, 512)
         y_interleave(0, 0, 512, "S")
-        for a, bk in [(2, 4), (3, 5)]:
-            for c in range(NG):
-                rows_matmul(2, 0, a, c, bk)
-            rows_out(2, 0, a, bk, "S")
         for t, bk in enumerate([0, 1, 2, 3]):
+            layer_matmul(1, t, 1, bk)
             bias_out(1, t, bk)
+        rows_bank(2, 0, 1, 4)
+        rows_bank(2, 0, 2, 5)
+        rows_bank(2, 0, 3, 6)
         relu_add(1, 0, 2, 0, 512)
-        cols_matmul(2, 1, 0, 6)
-        cols_matmul(2, 1, 1, 7)
-        rows_turn(2, 0, 0, 0)
-        rows_turn(2, 0, 1, 1)
-        rows_turn_out(2, 0, 0, 0, "S")
-        rows_turn_out(2, 0, 1, 1, "S")
-        cols_matmul(2, 1, 2, 2)
-        cols_matmul(2, 1, 3, 3)
-        relu_add(1, 2, 4, 0, 512)
-        store_y(1, 0, 512)
-        y_interleave(1, 0, 512, "S")
-        cols_out(2, 1, 0, 6)
         y_quantize(0, 0, 512)
         store_codes(0, 0, 512)
         for q in range(4):
             store_scales(0, q, "SP")
-        cols_out(2, 1, 1, 7)
+        relu_add(1, 2, 4, 0, 512)
+        store_y(1, 0, 512)
+        cols_matmul(2, 1, 0, 7)
+        rows_turn(2, 0, 0, 0)
+        rows_turn(2, 0, 1, 1)
+        rows_turn_out(2, 0, 0, 0, "S")
+        rows_turn_out(2, 0, 1, 1, "S")
+        y_interleave(1, 0, 512, "S")
+        cols_matmul(2, 1, 1, 2)
+        cols_matmul(2, 1, 2, 3)
+        cols_matmul(2, 1, 3, 4)
+        cols_out(2, 1, 0, 7)
+        cols_out(2, 1, 1, 2)
         h_quantize(2, 0, 0, 4)
-        cols_out(2, 1, 2, 2)
-        cols_out(2, 1, 3, 3)
+        cols_out(2, 1, 2, 3)
+        cols_out(2, 1, 3, 4)
 
-        last = [4, 5, 0, 1]
+        last = [5, 6, 7, 0]
+        wide = [(2, 1), (3, 2)]
+        turn = [3, 4]
         for t, bk in enumerate(last):
             layer_matmul(2, t, 0, bk)
-        for t, bk in enumerate(last):
+        for dt, bk in wide:
+            layer_t_matmul(2, dt, 0, bk)
+        for t in range(4):
             h_quantize(2, 1, t, t + 1)
-            layer_matmul(2, t, 1, bk)
+        layer_matmul(2, 0, 1, last[0])
+        layer_matmul(2, 1, 1, last[1])
+        for dt, bk in wide:
+            layer_t_matmul(2, dt, 1, bk)
+            layer_t_out(dt, bk)
+        layer_matmul(2, 2, 1, last[2])
+        layer_matmul(2, 3, 1, last[3])
         y_quantize(1, 0, 512)
         store_codes(1, 0, 512)
         for q in range(4):
             store_scales(1, q, "SP")
         for t, bk in enumerate(last):
             bias_out(2, t, bk, 0, 256)
-        bias_out(2, 0, last[0], 256, 512)
-        relu_add(2, 0, 4, 0, 256)
-        store_y(2, 0, 256)
-        y_interleave(2, 0, 256, "S")
-        for t in range(1, 4):
-            bias_out(2, t, last[t], 256, 512)
-        chunks = [(256, 384), (384, 448), (448, 512)]
-        for d0, d1 in chunks:
-            relu_add(2, 0, 4, d0, d1)
-            y_interleave(2, d0, d1, "S")
+        for (dt, bk), tbk in zip(wide, turn):
+            layer_t_turn(dt, tbk)
+        add_out(2, 2, turn[0])
+        y_interleave(2, 256, 384, "S")
+        add_out(2, 3, turn[1])
         store_y(2, 256, 512)
-        y_quantize(2, 0, 256)
-        store_codes(2, 0, 256)
-        for d0, d1 in chunks:
-            y_quantize(2, d0, d1)
+        y_interleave(2, 384, 512, "S")
+        relu_add(2, 0, 4, 0, 128)
+        y_interleave(2, 0, 128, "S")
+        relu_add(2, 0, 4, 128, 256)
+        store_y(2, 0, 256)
+        y_quantize(2, 256, 512)
         store_codes(2, 256, 512)
+        y_interleave(2, 128, 256, "V")
+        y_quantize(2, 0, 128)
+        y_quantize(2, 128, 256)
+        store_codes(2, 0, 256)
         for q in range(4):
             store_scales(2, q, "SP" if q < 2 else "S")

@@ -48,6 +48,7 @@ def tile_item_graph_propagation_h1_kernel(
         vec_rows = sbuf("vec_rows", [P, P], BF16)
         vec_cols = sbuf("vec_cols", [P, 16], BF16)
         deg_cols = sbuf("deg_cols", [P, 16], F32)
+        b_cols = sbuf("b_cols", [P, 2, 2], BF16)
         vec_all = sbuf("vec_all", [P, I + D], BF16)
         ident_bf = sbuf("ident_bf", [P, P], BF16)
         ident_f32 = sbuf("ident_f32", [P, P], F32)
@@ -74,14 +75,14 @@ def tile_item_graph_propagation_h1_kernel(
                 nc.scalar.copy(out=out, in_=in_)
 
         def setup():
+            nc.gpsimd.memset(s_scales[0][:].bitcast(I32), 0)
             nc.vector.memset(vec_rows[:], 0.0)
-            for plane in s_scales:
+            for plane in s_scales[1:]:
                 nc.vector.memset(plane[:].bitcast(I32), 0)
             nc.vector.memset(w_plane[:].bitcast(I32), 0)
             deg_rows = deg_scale.rearrange("(a p) -> a p", p=P)
             nc.scalar.dma_start(out=vec_rows[0:8, :], in_=deg_rows[0:8, :])
             nc.scalar.dma_start(out=vec_rows[8:12, :], in_=deg_rows[8:12, :])
-            nc.scalar.dma_start(out=vec_rows[12:16, :], in_=b.rearrange("(a p) -> a p", p=P))
             make_identity(nc, ident_bf[:])
             nc.scalar.activation(out=ident_f32[:], in_=ident_bf[:], func=ACT.Copy)
 
@@ -89,9 +90,14 @@ def tile_item_graph_propagation_h1_kernel(
             src = x[K * c : K * (c + 1), K * fg : K * (fg + 1)]
             nc.sync.dma_start(out=x_raw[fg, c][:], in_=src.rearrange("(p j) f -> p j f", j=4))
 
-        def load_s_words(g):
-            src = adj_words[:, :, 2 * K * g : 2 * K * (g + 1)].rearrange("c p n -> p c n")
-            nc.sync.dma_start(out=s_words[g][:].bitcast(I32), in_=src.bitcast(I32))
+        def load_s_words(g, c0=0, c1=NG, a0=0, a1=4):
+            n0 = 2 * K * g
+            src = adj_words[c0:c1, :, n0 + 2 * P * a0 : n0 + 2 * P * a1].rearrange("c p n -> p c n")
+            nc.sync.dma_start(out=s_words[g][:, c0:c1, 2 * P * a0 : 2 * P * a1].bitcast(I32), in_=src.bitcast(I32))
+
+        def load_b_cols():
+            with nc.allow_non_contiguous_dma(reason="one bias value to a partition"):
+                nc.sync.dma_start(out=b_cols[:, :, 0:1], in_=b[D // 2 : D].rearrange("(a p o) -> p a o", p=P, o=1))
 
         def load_plane(plane, src):
             for q in range(4):
@@ -224,7 +230,7 @@ def tile_item_graph_propagation_h1_kernel(
             )
 
         def layer_t_out(dt, bk):
-            nc.scalar.activation(out=r_cols[dt][:], in_=bank[bk][:], func=ACT.Relu, bias=deg_cols[:, 12 + dt : 13 + dt])
+            nc.scalar.activation(out=r_cols[dt][:], in_=bank[bk][:], func=ACT.Relu, bias=b_cols[:, dt - 2, 0:1])
 
         def layer_t_turn(dt, bk):
             for t in range(4):
@@ -259,8 +265,8 @@ def tile_item_graph_propagation_h1_kernel(
 
         setup()
         load_x(0, 0)
-        load_s_words(0)
         load_s_scales(0)
+        load_s_words(0)
         load_x(0, 1)
         load_x(0, 2)
         load_s_words(1)
@@ -275,6 +281,7 @@ def tile_item_graph_propagation_h1_kernel(
         load_spread(2 * K, deg_scale[2 * K : I])
         load_e(1)
         load_e(2)
+        load_b_cols()
 
         vec_turn(7)
         vec_turn_out(7)
@@ -309,7 +316,6 @@ def tile_item_graph_propagation_h1_kernel(
         rows_turn_out(0, 0, 0, 2, "S")
         rows_turn_out(0, 0, 1, 3, "S")
         cols_out(0, 1, 0, 0)
-        h_quantize(1, 0, 0, 4)
         cols_out(0, 1, 1, 1)
         cols_matmul(0, 1, 2, 4)
         cols_matmul(0, 1, 3, 5)
@@ -326,6 +332,7 @@ def tile_item_graph_propagation_h1_kernel(
         for t, bk in enumerate([7, 0, 1, 2]):
             layer_matmul(0, t, 0, bk)
         h_quantize(0, 1, 0, 4)
+        h_quantize(1, 0, 0, 4)
         for t, bk in enumerate([7, 0, 1, 2]):
             layer_matmul(0, t, 1, bk)
             bias_out(0, t, bk)
@@ -338,11 +345,12 @@ def tile_item_graph_propagation_h1_kernel(
         cols_out(1, 1, 2, 4)
         relu_add(0, 1, 2, 0, 512)
         cols_out(1, 1, 3, 6)
-        relu_add(0, 2, 3, 0, 512)
+        relu_add(0, 2, 3, 0, 256)
         rows_bank(2, 0, 0, 7)
         for t, bk in enumerate([0, 1, 2, 3]):
             layer_matmul(1, t, 0, bk)
         h_quantize(1, 1, 0, 4)
+        relu_add(0, 2, 3, 256, 512)
         relu_add(0, 3, 4, 0, 512)
         store_y(0, 0, 512)
         y_interleave(0, 0, 512, "S")
@@ -364,7 +372,8 @@ def tile_item_graph_propagation_h1_kernel(
         rows_turn(2, 0, 1, 1)
         rows_turn_out(2, 0, 0, 0, "S")
         rows_turn_out(2, 0, 1, 1, "S")
-        y_interleave(1, 0, 512, "S")
+        y_interleave(1, 0, 256, "S")
+        y_interleave(1, 256, 512, "S")
         cols_matmul(2, 1, 1, 2)
         cols_matmul(2, 1, 2, 3)
         cols_matmul(2, 1, 3, 4)
@@ -372,46 +381,46 @@ def tile_item_graph_propagation_h1_kernel(
         cols_out(2, 1, 1, 2)
         h_quantize(2, 0, 0, 4)
         cols_out(2, 1, 2, 3)
+        y_quantize(1, 0, 256)
         cols_out(2, 1, 3, 4)
+        y_quantize(1, 256, 512)
+        store_codes(1, 0, 512)
+        for q in range(4):
+            store_scales(1, q, "SP")
 
         last = [5, 6, 7, 0]
         wide = [(2, 1), (3, 2)]
         turn = [3, 4]
         for t, bk in enumerate(last):
             layer_matmul(2, t, 0, bk)
-        for dt, bk in wide:
-            layer_t_matmul(2, dt, 0, bk)
-        for t in range(4):
+        layer_t_matmul(2, wide[0][0], 0, wide[0][1])
+        for t, bk in enumerate(last):
             h_quantize(2, 1, t, t + 1)
-        layer_matmul(2, 0, 1, last[0])
-        layer_matmul(2, 1, 1, last[1])
-        for dt, bk in wide:
-            layer_t_matmul(2, dt, 1, bk)
-            layer_t_out(dt, bk)
-        layer_matmul(2, 2, 1, last[2])
-        layer_matmul(2, 3, 1, last[3])
-        y_quantize(1, 0, 512)
-        store_codes(1, 0, 512)
-        for q in range(4):
-            store_scales(1, q, "SP")
+            layer_matmul(2, t, 1, bk)
+        layer_t_matmul(2, wide[0][0], 1, wide[0][1])
+        layer_t_out(*wide[0])
+        layer_t_matmul(2, wide[1][0], 0, wide[1][1])
+        layer_t_matmul(2, wide[1][0], 1, wide[1][1])
+        layer_t_out(*wide[1])
+
         for t, bk in enumerate(last):
             bias_out(2, t, bk, 0, 256)
         for (dt, bk), tbk in zip(wide, turn):
             layer_t_turn(dt, tbk)
-        add_out(2, 2, turn[0])
-        y_interleave(2, 256, 384, "S")
-        add_out(2, 3, turn[1])
-        store_y(2, 256, 512)
-        y_interleave(2, 384, 512, "S")
         relu_add(2, 0, 4, 0, 128)
         y_interleave(2, 0, 128, "S")
         relu_add(2, 0, 4, 128, 256)
         store_y(2, 0, 256)
-        y_quantize(2, 256, 512)
-        store_codes(2, 256, 512)
-        y_interleave(2, 128, 256, "V")
-        y_quantize(2, 0, 128)
-        y_quantize(2, 128, 256)
+        y_interleave(2, 128, 256, "S")
+        add_out(2, 2, turn[0])
+        y_interleave(2, 256, 384, "S")
+        add_out(2, 3, turn[1])
+        store_y(2, 256, 512)
+        y_quantize(2, 0, 256)
         store_codes(2, 0, 256)
+        y_interleave(2, 384, 512, "V")
+        y_quantize(2, 256, 384)
+        y_quantize(2, 384, 512)
+        store_codes(2, 256, 512)
         for q in range(4):
             store_scales(2, q, "SP" if q < 2 else "S")

@@ -122,8 +122,12 @@ def tile_item_graph_propagation_h1_kernel(
             src = x_raw[fg, c][:].rearrange("p j (n h t) -> p n t h j", h=2, t=4)[:, :, t0:t1, :, :]
             copy_on(eng, out, src)
 
-        def x_quantize(fg, c):
-            nc.vector.quantize_mx(out=x_codes[fg, c][:].bitcast(FP8X4), scales=x_scales[fg, c][:], in_=x_il[fg, c][:])
+        def x_quantize(fg, c, t0=0, t1=4):
+            nc.vector.quantize_mx(
+                out=x_codes[fg, c][:, P * t0 : P * t1].bitcast(FP8X4),
+                scales=x_scales[fg, c][:, P * t0 : P * t1],
+                in_=x_il[fg, c][:, K * t0 : K * t1],
+            )
 
         def vec_turn(bk):
             nc.tensor.transpose(bank[bk][:].bitcast(BF16)[:, 0:P], vec_rows[:], ident_bf[:])
@@ -250,9 +254,9 @@ def tile_item_graph_propagation_h1_kernel(
                 out=y_codes[g][:, d0:d1].bitcast(FP8X4), scales=y_scales[g][:, d0:d1], in_=y_il[g][:, 4 * d0 : 4 * d1]
             )
 
-        def store_y(g, d0, d1):
+        def store_y(g, d0, d1, t0=0, t1=4):
             dst = out_0[K * g : K * (g + 1), d0:d1].rearrange("(p t) d -> p t d", t=4)
-            nc.sync.dma_start(out=dst, in_=y_sb[g][:, :, d0:d1])
+            nc.sync.dma_start(out=dst[:, t0:t1, :], in_=y_sb[g][:, t0:t1, d0:d1])
 
         def store_codes(g, d0, d1):
             dst = out_1[g].rearrange("p m t -> p (m t)")[:, 4 * d0 : 4 * d1]
@@ -269,8 +273,8 @@ def tile_item_graph_propagation_h1_kernel(
         load_s_words(0)
         load_x(0, 1)
         load_x(0, 2)
-        load_s_words(1)
         load_s_scales(1)
+        load_s_words(1)
         for c in range(NG):
             load_x(1, c)
         load_w()
@@ -292,7 +296,8 @@ def tile_item_graph_propagation_h1_kernel(
         for c in range(1, NG):
             x_interleave(0, c, "V", 0, 2)
             x_interleave(0, c, "S", 2, 4)
-            x_quantize(0, c)
+            x_quantize(0, c, 0, 2)
+            x_quantize(0, c, 2, 4)
         vec_spread_out(0, 8, 7)
         for c in range(NG):
             for a in range(4):
@@ -304,7 +309,8 @@ def tile_item_graph_propagation_h1_kernel(
             x_interleave(1, c, "S", 2, 4)
             if c > 0:
                 x_quantize(1, c - 1)
-        x_quantize(1, 2)
+        x_quantize(1, 2, 0, 2)
+        x_quantize(1, 2, 2, 4)
         for a in range(4):
             rows_out(0, 0, a, a, "S")
         for a in range(4):
@@ -317,6 +323,7 @@ def tile_item_graph_propagation_h1_kernel(
         rows_turn_out(0, 0, 1, 3, "S")
         cols_out(0, 1, 0, 0)
         cols_out(0, 1, 1, 1)
+        h_quantize(1, 0, 0, 4)
         cols_matmul(0, 1, 2, 4)
         cols_matmul(0, 1, 3, 5)
         h_quantize(0, 0, 0, 4)
@@ -331,8 +338,8 @@ def tile_item_graph_propagation_h1_kernel(
         rows_bank(1, 1, 0, 6)
         for t, bk in enumerate([7, 0, 1, 2]):
             layer_matmul(0, t, 0, bk)
-        h_quantize(0, 1, 0, 4)
-        h_quantize(1, 0, 0, 4)
+        h_quantize(0, 1, 0, 2)
+        h_quantize(0, 1, 2, 4)
         for t, bk in enumerate([7, 0, 1, 2]):
             layer_matmul(0, t, 1, bk)
             bias_out(0, t, bk)
@@ -403,22 +410,26 @@ def tile_item_graph_propagation_h1_kernel(
         layer_t_matmul(2, wide[1][0], 1, wide[1][1])
         layer_t_out(*wide[1])
 
-        for t, bk in enumerate(last):
-            bias_out(2, t, bk, 0, 256)
+        for t in range(3):
+            bias_out(2, t, last[t], 0, 256)
+        relu_add(2, 0, 2, 0, 256)
+        store_y(2, 0, 256, 0, 2)
+        bias_out(2, 3, last[3], 0, 256)
         for (dt, bk), tbk in zip(wide, turn):
             layer_t_turn(dt, tbk)
-        relu_add(2, 0, 4, 0, 128)
+        relu_add(2, 2, 4, 0, 256)
+        store_y(2, 0, 256, 2, 4)
         y_interleave(2, 0, 128, "S")
-        relu_add(2, 0, 4, 128, 256)
-        store_y(2, 0, 256)
         y_interleave(2, 128, 256, "S")
         add_out(2, 2, turn[0])
+        store_y(2, 256, 384)
         y_interleave(2, 256, 384, "S")
         add_out(2, 3, turn[1])
-        store_y(2, 256, 512)
-        y_quantize(2, 0, 256)
-        store_codes(2, 0, 256)
+        store_y(2, 384, 512)
+        y_quantize(2, 0, 128)
         y_interleave(2, 384, 512, "V")
+        y_quantize(2, 128, 256)
+        store_codes(2, 0, 256)
         y_quantize(2, 256, 384)
         y_quantize(2, 384, 512)
         store_codes(2, 256, 512)

from contextlib import ExitStack

import concourse.mybir as mybir
from concourse.masks import make_identity

I, F, D = 1536, 1024, 512
FLOPS = 2 * I * I * F + 2 * I * F * D

F32 = mybir.dt.float32
BF16 = mybir.dt.bfloat16
I32 = mybir.dt.int32
U32 = mybir.dt.uint32
U8 = mybir.dt.uint8
FP8X4 = mybir.dt.float8_e4m3fn_x4
FP4X4 = mybir.dt.float4_e2m1fn_x4
ALU = mybir.AluOpType
ACT = mybir.ActivationFunctionType

P = 128
K = 512
NG = I // K
NF = F // K
ROW_UNITS = [(0, 0), (1, 1), (2, 0)]


def tile_item_graph_propagation_h1_kernel(
    tc, adj_words, adj_scales, x, deg_scale, w_words, w_scales, b, e, out_0, out_1, out_2
):
    nc = tc.nc
    with ExitStack() as ctx:
        sb = ctx.enter_context(tc.tile_pool(name="sb", bufs=1))
        ps = ctx.enter_context(tc.psum_pool(name="ps", bufs=1))
        ctx.enter_context(tc.manual_schedule())

        def sbuf(name, shape, dtype):
            return sb.tile(shape, dtype, name=name, align_bytes=64)

        bank = [ps.tile([P, 512], F32, name="bank%d" % i) for i in range(8)]
        pairs = [(fg, c) for fg in range(NF) for c in range(NG)]
        x_raw = {k: sbuf("x_raw%d%d" % k, [P, 4, K], BF16) for k in pairs}
        x_il = {k: sbuf("x_il%d%d" % k, [P, 4 * K], BF16) for k in pairs}
        x_codes = {k: sbuf("x_codes%d%d" % k, [P, K], U32) for k in pairs}
        x_scales = {k: sbuf("x_scales%d%d" % k, [P, K], U8) for k in pairs}
        s_words = [sbuf("s_words%d" % g, [P, NG, 2 * K], U8) for g in range(NG)]
        s_scales = [sbuf("s_scales%d" % g, [P, NG, K], U8) for g in range(NG)]
        w_codes = sbuf("w_codes", [P, NF, 2 * D], U8)
        w_plane = sbuf("w_plane", [P, NF, D], U8)
        vec_rows = sbuf("vec_rows", [P, P], BF16)
        vec_cols = sbuf("vec_cols", [P, 16], BF16)
        deg_cols = sbuf("deg_cols", [P, 16], F32)
        b_cols = sbuf("b_cols", [P, 2, 2], BF16)
        vec_all = sbuf("vec_all", [P, I + D], BF16)
        ident_bf = sbuf("ident_bf", [P, P], BF16)
        ident_f32 = sbuf("ident_f32", [P, P], F32)
        units = [(g, fg) for g in range(NG) for fg in range(NF)]
        h_il = {k: sbuf("h_il%d%d" % k, [P, 4 * K], BF16) for k in units}
        h_codes = {k: sbuf("h_codes%d%d" % k, [P, K], U32) for k in units}
        h_scales = {k: sbuf("h_scales%d%d" % k, [P, K], U8) for k in units}
        h_rows = {k: [sbuf("h_rows%d%d%d" % (k + (a,)), [P, K], BF16) for a in range(4)] for k in ROW_UNITS}
        r_cols = [sbuf("r_cols%d" % dt, [P, K], F32) for dt in range(4)]
        e_sb = [sbuf("e_sb%d" % g, [P, 4, D], BF16) for g in range(NG)]
        y_sb = [sbuf("y_sb%d" % g, [P, 4, D], F32) for g in range(NG)]
        y_il = [sbuf("y_il%d" % g, [P, 4 * D], BF16) for g in range(NG)]
        y_codes = [sbuf("y_codes%d" % g, [P, D], U32) for g in range(NG)]
        y_scales = [sbuf("y_scales%d" % g, [P, D], U8) for g in range(NG)]

        def s_operand(g, c, a):
            words = s_words[g][:, c, 2 * P * a : 2 * P * (a + 1)].bitcast(FP4X4)
            return words, s_scales[g][:, c, P * a : P * (a + 1)]

        def copy_on(eng, out, in_):
            if eng == "V":
                nc.vector.tensor_copy(out=out, in_=in_)
            else:
                nc.scalar.copy(out=out, in_=in_)

        def setup():
            nc.gpsimd.memset(s_scales[0][:].bitcast(I32), 0)
            nc.vector.memset(vec_rows[:], 0.0)
            for plane in s_scales[1:]:
                nc.vector.memset(plane[:].bitcast(I32), 0)
            nc.vector.memset(w_plane[:].bitcast(I32), 0)
            deg_rows = deg_scale.rearrange("(a p) -> a p", p=P)
            nc.scalar.dma_start(out=vec_rows[0:8, :], in_=deg_rows[0:8, :])
            nc.scalar.dma_start(out=vec_rows[8:12, :], in_=deg_rows[8:12, :])
            make_identity(nc, ident_bf[:])
            nc.scalar.activation(out=ident_f32[:], in_=ident_bf[:], func=ACT.Copy)

        def load_x(fg, c):
            src = x[K * c : K * (c + 1), K * fg : K * (fg + 1)]
            nc.sync.dma_start(out=x_raw[fg, c][:], in_=src.rearrange("(p j) f -> p j f", j=4))

        def load_s_words(g, c0=0, c1=NG, a0=0, a1=4):
            n0 = 2 * K * g
            src = adj_words[c0:c1, :, n0 + 2 * P * a0 : n0 + 2 * P * a1].rearrange("c p n -> p c n")
            nc.sync.dma_start(out=s_words[g][:, c0:c1, 2 * P * a0 : 2 * P * a1].bitcast(I32), in_=src.bitcast(I32))

        def load_b_cols():
            with nc.allow_non_contiguous_dma(reason="one bias value to a partition"):
                nc.sync.dma_start(out=b_cols[:, :, 0:1], in_=b[D // 2 : D].rearrange("(a p o) -> p a o", p=P, o=1))

        def load_plane(plane, src):
            for q in range(4):
                rows = src[:, 4 * q : 4 * q + 4, :].rearrange("c r n -> r c n")
                nc.sync.dma_start(out=plane[32 * q : 32 * q + 4, :, :].bitcast(I32), in_=rows.bitcast(I32))

        def load_s_scales(g):
            load_plane(s_scales[g], adj_scales[:, :, K * g : K * (g + 1)])

        def load_spread(n0, vec):
            nc.sync.dma_start(out=vec_all[:, n0 : n0 + K], in_=vec.partition_broadcast(P))

        def load_w():
            nc.sync.dma_start(out=w_codes[:].bitcast(I32), in_=w_words.rearrange("c p n -> p c n").bitcast(I32))
            load_plane(w_plane, w_scales)

        def load_e(g):
            nc.sync.dma_start(out=e_sb[g][:], in_=e[K * g : K * (g + 1), :].rearrange("(p t) d -> p t d", t=4))

        def x_interleave(fg, c, eng, t0, t1):
            out = x_il[fg, c][:, K * t0 : K * t1].rearrange("p (t n h j) -> p n t h j", n=64, h=2, j=4)
            src = x_raw[fg, c][:].rearrange("p j (n h t) -> p n t h j", h=2, t=4)[:, :, t0:t1, :, :]
            copy_on(eng, out, src)

        def x_quantize(fg, c, t0=0, t1=4):
            nc.vector.quantize_mx(
                out=x_codes[fg, c][:, P * t0 : P * t1].bitcast(FP8X4),
                scales=x_scales[fg, c][:, P * t0 : P * t1],
                in_=x_il[fg, c][:, K * t0 : K * t1],
            )

        def vec_turn(bk):
            nc.tensor.transpose(bank[bk][:].bitcast(BF16)[:, 0:P], vec_rows[:], ident_bf[:])

        def vec_turn_out(bk):
            nc.scalar.copy(out=deg_cols[:], in_=bank[bk][:].bitcast(BF16)[:, 0:16])
            nc.scalar.copy(out=vec_cols[:], in_=bank[bk][:].bitcast(BF16)[:, 0:16])

        def vec_spread(c0, c1, bk):
            for i in range(c1 - c0):
                col = vec_cols[:, c0 + i : c0 + i + 1].to_broadcast([P, P])
                nc.tensor.transpose(bank[bk][:].bitcast(BF16)[:, P * i : P * (i + 1)], col, ident_bf[:])

        def vec_spread_out(c0, c1, bk):
            nc.scalar.copy(out=vec_all[:, P * c0 : P * c1], in_=bank[bk][:].bitcast(BF16)[:, 0 : P * (c1 - c0)])

        def cols_matmul(g, fg, a, bk):
            for j in range(4):
                for c in range(NG):
                    words, scales = s_operand(g, c, a)
                    nc.tensor.matmul_mx(
                        out=bank[bk][:, P * j : P * (j + 1)],
                        lhsT=x_codes[fg, c][:, P * j : P * (j + 1)].bitcast(FP8X4),
                        lhsT_scale=x_scales[fg, c][:, P * j : P * (j + 1)],
                        rhs=words,
                        rhs_scale=scales,
                        start=(c == 0),
                        stop=(c == NG - 1),
                    )

        def cols_out(g, fg, a, bk):
            out = h_il[g, fg][:].rearrange("p (t m j) -> p t m j", t=4, j=4)[:, :, 32 * a : 32 * (a + 1), :]
            acc = bank[bk][:].rearrange("p (j m t) -> p t m j", j=4, t=4)
            n0 = K * g + P * a
            deg = vec_all[:, n0 : n0 + P].rearrange("p (m t o) -> p t m o", t=4, o=1).to_broadcast([P, 4, 32, 4])
            nc.vector.tensor_tensor(out=out, in0=acc, in1=deg, op=ALU.mult)

        def rows_matmul(g, fg, a, c, bk):
            words, scales = s_operand(g, c, a)
            nc.tensor.matmul_mx(
                out=bank[bk][:],
                lhsT=words,
                lhsT_scale=scales,
                rhs=x_codes[fg, c][:].bitcast(FP8X4),
                rhs_scale=x_scales[fg, c][:],
                start=(c == 0),
                stop=(c == NG - 1),
            )

        def rows_out(g, fg, a, bk, eng):
            out = h_rows[g, fg][a][:].rearrange("p (u m v) -> p u m v", u=2, v=2)
            acc = bank[bk][:].rearrange("p (u v m) -> p u m v", u=2, v=2)
            deg = deg_cols[:, 4 * g + a : 4 * g + a + 1]
            if eng == "V":
                nc.vector.tensor_scalar(out=out, in0=acc, scalar1=deg, scalar2=None, op0=ALU.mult)
            else:
                nc.scalar.activation(out=out, in_=acc, func=ACT.Copy, scale=deg)

        def rows_turn(g, fg, half, bk):
            for a2 in range(2):
                words = h_rows[g, fg][2 * half + a2][:].bitcast(F32)
                for u in range(2):
                    n0 = 2 * P * u + P * a2
                    nc.tensor.transpose(bank[bk][:, n0 : n0 + P], words[:, P * u : P * (u + 1)], ident_f32[:])

        def rows_turn_out(g, fg, half, bk, eng):
            out = h_il[g, fg][:].bitcast(F32).rearrange("p (t m u) -> p t m u", t=4, u=2)[:, :, 64 * half : 64 * (half + 1), :]
            copy_on(eng, out, bank[bk][:].rearrange("p (u m t) -> p t m u", u=2, t=4))

        def h_quantize(g, fg, t0, t1):
            nc.vector.quantize_mx(
                out=h_codes[g, fg][:, P * t0 : P * t1].bitcast(FP8X4),
                scales=h_scales[g, fg][:, P * t0 : P * t1],
                in_=h_il[g, fg][:, K * t0 : K * t1],
            )

        def layer_matmul(g, t, fg, bk):
            nc.tensor.matmul_mx(
                out=bank[bk][:],
                lhsT=h_codes[g, fg][:, P * t : P * (t + 1)].bitcast(FP8X4),
                lhsT_scale=h_scales[g, fg][:, P * t : P * (t + 1)],
                rhs=w_codes[:, fg, :].bitcast(FP4X4),
                rhs_scale=w_plane[:, fg, :],
                start=(fg == 0),
                stop=(fg == NF - 1),
            )

        def bias_out(g, t, bk, d0=0, d1=D):
            nc.vector.tensor_tensor(out=y_sb[g][:, t, d0:d1], in0=bank[bk][:, d0:d1], in1=vec_all[:, I + d0 : I + d1], op=ALU.add)

        def relu_add(g, t0, t1, d0, d1):
            y = y_sb[g][:, t0:t1, d0:d1]
            nc.vector.scalar_tensor_tensor(out=y, in0=y, scalar=0.0, in1=e_sb[g][:, t0:t1, d0:d1], op0=ALU.max, op1=ALU.add)

        def layer_t_matmul(g, dt, fg, bk):
            nc.tensor.matmul_mx(
                out=bank[bk][:],
                lhsT=w_codes[:, fg, 2 * P * dt : 2 * P * (dt + 1)].bitcast(FP4X4),
                lhsT_scale=w_plane[:, fg, P * dt : P * (dt + 1)],
                rhs=h_codes[g, fg][:].bitcast(FP8X4),
                rhs_scale=h_scales[g, fg][:],
                start=(fg == 0),
                stop=(fg == NF - 1),
            )

        def layer_t_out(dt, bk):
            nc.scalar.activation(out=r_cols[dt][:], in_=bank[bk][:], func=ACT.Relu, bias=b_cols[:, dt - 2, 0:1])

        def layer_t_turn(dt, bk):
            for t in range(4):
                nc.tensor.transpose(bank[bk][:, P * t : P * (t + 1)], r_cols[dt][:, P * t : P * (t + 1)], ident_f32[:])

        def add_out(g, dt, bk):
            cols = slice(P * dt, P * (dt + 1))
            acc = bank[bk][:].rearrange("p (t d) -> p t d", t=4)
            nc.vector.tensor_tensor(out=y_sb[g][:, :, cols], in0=acc, in1=e_sb[g][:, :, cols], op=ALU.add)

        def y_interleave(g, d0, d1, eng):
            out = y_il[g][:, 4 * d0 : 4 * d1].rearrange("p (n i t) -> p n t i", i=4, t=4)
            copy_on(eng, out, y_sb[g][:, :, d0:d1].rearrange("p t (n i) -> p n t i", i=4))

        def y_quantize(g, d0, d1):
            nc.vector.quantize_mx(
                out=y_codes[g][:, d0:d1].bitcast(FP8X4), scales=y_scales[g][:, d0:d1], in_=y_il[g][:, 4 * d0 : 4 * d1]
            )

        def store_y(g, d0, d1, t0=0, t1=4):
            dst = out_0[K * g : K * (g + 1), d0:d1].rearrange("(p t) d -> p t d", t=4)
            nc.sync.dma_start(out=dst[:, t0:t1, :], in_=y_sb[g][:, t0:t1, d0:d1])

        def store_codes(g, d0, d1):
            dst = out_1[g].rearrange("p m t -> p (m t)")[:, 4 * d0 : 4 * d1]
            nc.sync.dma_start(out=dst.bitcast(I32), in_=y_codes[g][:, d0:d1].bitcast(I32))

        def store_scales(g, q, eng):
            queue = nc.sync if eng == "SP" else nc.scalar
            queue.dma_start(out=out_2[g, 4 * q : 4 * q + 4, :].bitcast(I32), in_=y_scales[g][32 * q : 32 * q + 4, :].bitcast(I32))


        setup()
        load_x(0, 0)
        load_s_scales(0)
        load_s_words(0)
        load_x(0, 1)
        load_x(0, 2)
        load_s_scales(1)
        load_s_words(1)
        for c in range(NG):
            load_x(1, c)
        load_w()
        load_spread(I, b)
        load_e(0)
        load_s_words(2)
        load_s_scales(2)
        load_spread(2 * K, deg_scale[2 * K : I])
        load_e(1)
        load_e(2)
        load_b_cols()

        vec_turn(7)
        vec_turn_out(7)
        vec_spread(0, 8, 7)
        x_interleave(0, 0, "V", 0, 3)
        x_interleave(0, 0, "S", 3, 4)
        x_quantize(0, 0)
        for c in range(1, NG):
            x_interleave(0, c, "V", 0, 2)
            x_interleave(0, c, "S", 2, 4)
            x_quantize(0, c, 0, 2)
            x_quantize(0, c, 2, 4)
        vec_spread_out(0, 8, 7)
        for c in range(NG):
            for a in range(4):
                rows_matmul(0, 0, a, c, a)
        for a in range(4):
            cols_matmul(1, 0, a, 4 + a)
        for c in range(NG):
            x_interleave(1, c, "V", 0, 2)
            x_interleave(1, c, "S", 2, 4)
            if c > 0:
                x_quantize(1, c - 1)
        x_quantize(1, 2, 0, 2)
        x_quantize(1, 2, 2, 4)
        for a in range(4):
            rows_out(0, 0, a, a, "S")
        for a in range(4):
            cols_out(1, 0, a, 4 + a)
        cols_matmul(0, 1, 0, 0)
        cols_matmul(0, 1, 1, 1)
        rows_turn(0, 0, 0, 2)
        rows_turn(0, 0, 1, 3)
        rows_turn_out(0, 0, 0, 2, "S")
        rows_turn_out(0, 0, 1, 3, "S")
        cols_out(0, 1, 0, 0)
        cols_out(0, 1, 1, 1)
        h_quantize(1, 0, 0, 4)
        cols_matmul(0, 1, 2, 4)
        cols_matmul(0, 1, 3, 5)
        h_quantize(0, 0, 0, 4)
        cols_out(0, 1, 2, 4)
        cols_out(0, 1, 3, 5)

        def rows_bank(g, fg, a, bk):
            for c in range(NG):
                rows_matmul(g, fg, a, c, bk)
            rows_out(g, fg, a, bk, "S")

        rows_bank(1, 1, 0, 6)
        for t, bk in enumerate([7, 0, 1, 2]):
            layer_matmul(0, t, 0, bk)
        h_quantize(0, 1, 0, 2)
        h_quantize(0, 1, 2, 4)
        for t, bk in enumerate([7, 0, 1, 2]):
            layer_matmul(0, t, 1, bk)
            bias_out(0, t, bk)
        rows_bank(1, 1, 1, 3)
        cols_matmul(1, 1, 2, 4)
        rows_turn(1, 1, 0, 5)
        rows_turn_out(1, 1, 0, 5, "S")
        cols_matmul(1, 1, 3, 6)
        relu_add(0, 0, 1, 0, 512)
        cols_out(1, 1, 2, 4)
        relu_add(0, 1, 2, 0, 512)
        cols_out(1, 1, 3, 6)
        relu_add(0, 2, 3, 0, 256)
        rows_bank(2, 0, 0, 7)
        for t, bk in enumerate([0, 1, 2, 3]):
            layer_matmul(1, t, 0, bk)
        h_quantize(1, 1, 0, 4)
        relu_add(0, 2, 3, 256, 512)
        relu_add(0, 3, 4, 0, 512)
        store_y(0, 0, 512)
        y_interleave(0, 0, 512, "S")
        for t, bk in enumerate([0, 1, 2, 3]):
            layer_matmul(1, t, 1, bk)
            bias_out(1, t, bk)
        rows_bank(2, 0, 1, 4)
        rows_bank(2, 0, 2, 5)
        rows_bank(2, 0, 3, 6)
        relu_add(1, 0, 2, 0, 512)
        y_quantize(0, 0, 512)
        store_codes(0, 0, 512)
        for q in range(4):
            store_scales(0, q, "SP")
        relu_add(1, 2, 4, 0, 512)
        store_y(1, 0, 512)
        cols_matmul(2, 1, 0, 7)
        rows_turn(2, 0, 0, 0)
        rows_turn(2, 0, 1, 1)
        rows_turn_out(2, 0, 0, 0, "S")
        rows_turn_out(2, 0, 1, 1, "S")
        y_interleave(1, 0, 256, "S")
        y_interleave(1, 256, 512, "S")
        cols_matmul(2, 1, 1, 2)
        cols_matmul(2, 1, 2, 3)
        cols_matmul(2, 1, 3, 4)
        cols_out(2, 1, 0, 7)
        cols_out(2, 1, 1, 2)
        h_quantize(2, 0, 0, 4)
        cols_out(2, 1, 2, 3)
        y_quantize(1, 0, 256)
        cols_out(2, 1, 3, 4)
        y_quantize(1, 256, 512)
        store_codes(1, 0, 512)
        for q in range(4):
            store_scales(1, q, "SP")

        last = [5, 6, 7, 0]
        wide = [(2, 1), (3, 2)]
        turn = [3, 4]
        for t, bk in enumerate(last):
            layer_matmul(2, t, 0, bk)
        layer_t_matmul(2, wide[0][0], 0, wide[0][1])
        for t, bk in enumerate(last):
            h_quantize(2, 1, t, t + 1)
            layer_matmul(2, t, 1, bk)
        layer_t_matmul(2, wide[0][0], 1, wide[0][1])
        layer_t_out(*wide[0])
        layer_t_matmul(2, wide[1][0], 0, wide[1][1])
        layer_t_matmul(2, wide[1][0], 1, wide[1][1])
        layer_t_out(*wide[1])

        for t in range(3):
            bias_out(2, t, last[t], 0, 256)
        relu_add(2, 0, 2, 0, 256)
        store_y(2, 0, 256, 0, 2)
        bias_out(2, 3, last[3], 0, 256)
        for (dt, bk), tbk in zip(wide, turn):
            layer_t_turn(dt, tbk)
        relu_add(2, 2, 4, 0, 256)
        store_y(2, 0, 256, 2, 4)
        y_interleave(2, 0, 128, "S")
        y_interleave(2, 128, 256, "S")
        add_out(2, 2, turn[0])
        store_y(2, 256, 384)
        y_interleave(2, 256, 384, "S")
        add_out(2, 3, turn[1])
        store_y(2, 384, 512)
        y_quantize(2, 0, 128)
        y_interleave(2, 384, 512, "V")
        y_quantize(2, 128, 256)
        store_codes(2, 0, 256)
        y_quantize(2, 256, 384)
        y_quantize(2, 384, 512)
        store_codes(2, 256, 512)
        for q in range(4):
            store_scales(2, q, "SP" if q < 2 else "S")
